import numpy as np
import ml_dtypes


def mxq(x, axis, fmt="e4m3"):
    dtype, down = {"e4m3": (ml_dtypes.float8_e4m3fn, 7), "e5m2": (ml_dtypes.float8_e5m2, 14)}[fmt]
    v = np.moveaxis(np.asarray(x, np.float32).astype(ml_dtypes.bfloat16).astype(np.float64), axis, -1)
    blocks = v.reshape(v.shape[:-1] + (-1, 32))
    amax = np.abs(blocks).max(-1, keepdims=True)
    byte = np.maximum(np.where(amax > 0, np.frexp(amax)[1] - 1 + 127, 0) - down, 1)
    scale = np.exp2(byte - 127.0)
    codes = (blocks / scale).astype(np.float32).astype(dtype).astype(np.float64)
    return np.moveaxis((codes * scale).reshape(v.shape), -1, axis)


WIDE = False


def mx_kscale(k):
    if not WIDE:
        return np.ones(k)
    levels = np.array([10, -10, 5, -5, 0])
    if k % 512:
        return np.exp2(np.random.permutation(np.resize(levels, k // 32))).repeat(32)
    a = np.empty((k // 512, 16))
    for p in range(k // 512):
        a[p, :8] = np.random.permutation(np.resize(levels, 8))
        for g in range(8):
            far = levels[np.abs(levels - a[p, g]) >= 10]
            a[p, g + 8] = far[np.random.randint(len(far))]
    return np.exp2(a.ravel()).repeat(32)


def f64(x):
    return np.asarray(x).astype(np.float64)


def striped(idx):
    return np.tile(np.asarray(idx).reshape(-1, 16).T, (8, 1)).astype(np.uint16)


def unstriped(offs):
    return offs[:16].T.reshape(-1).astype(np.int64)


E2M1 = np.array([0.0, 0.5, 1.0, 1.5, 2.0, 3.0, 4.0, 6.0, -0.0, -0.5, -1.0, -1.5, -2.0, -3.0, -4.0, -6.0])


def pack_weight(w, fmt):
    k, n = w.shape
    w = f64(np.asarray(w, np.float32).astype(ml_dtypes.bfloat16)).reshape(k // 32, 32, n)
    amax = np.abs(w).max(1)
    if fmt == "e4m3":
        byte = np.frexp(amax)[1] - 1 + 127 - 7
    else:
        mant, ex = np.frexp(amax / 6.0)
        byte = np.where(mant > 0.5, ex, ex - 1) + 127
    byte = np.clip(np.where(amax > 0, byte, 1), 1, 254)
    scaled = (w * np.exp2(127.0 - byte)[:, None, :]).reshape(k, n).astype(np.float32)
    by_word = np.ascontiguousarray(scaled.reshape(k // 512, 128, 4, n).transpose(0, 1, 3, 2))
    if fmt == "e4m3":
        words = by_word.astype(ml_dtypes.float8_e4m3fn).view(np.uint8)
    else:
        c = by_word.astype(ml_dtypes.float4_e2m1fn).view(np.uint8) & 0xF
        words = (c[..., 0::2] | (c[..., 1::2] << 4)).reshape(k // 512, 128, 2 * n)
    return np.ascontiguousarray(words), np.ascontiguousarray(byte.astype(np.uint8).reshape(k // 512, 16, n))


def unpack_weight(words, scales, fmt):
    g, _, n = scales.shape
    words = np.ascontiguousarray(words).reshape(g, 128, n, -1)
    if fmt == "e4m3":
        vals = words.view(ml_dtypes.float8_e4m3fn).astype(np.float64)
    else:
        nib = np.empty((g, 128, n, 4), np.uint8)
        nib[..., 0::2] = words & 0xF
        nib[..., 1::2] = words >> 4
        vals = E2M1[nib]
    vals = vals * np.repeat(np.exp2(scales.astype(np.float64) - 127.0), 8, axis=1)[..., None]
    return vals.transpose(0, 1, 3, 2).reshape(g * 512, n)


B, N, T, D, NQ = 1, 512, 2048, 512, 256


def setup_inputs():
    n = np.random.standard_normal
    idx = np.random.permutation(T)[:B * N]
    s = mx_kscale(D)[:, None]
    kp = pack_weight(n((D, T)) / s, "e4m3")
    cp = pack_weight(n((D, T)) / s / 12, "e4m3")
    return {
        "qT": (n((B, D, NQ)) * s * (1.00 / np.sqrt(D))).astype(np.float32),
        "k_words": kp[0],
        "k_scales": kp[1],
        "c_words": cp[0],
        "c_scales": cp[1],
        "kn": np.tile(np.random.uniform(1.0, 4.0, 2048), (128, 1)).astype(np.float32),
        "qn": (np.random.uniform(1.0, 4.0, (B, NQ, 1))).astype(np.float32),
        "offs": striped(idx),
    }


def reference(qT, k_words, k_scales, c_words, c_scales, kn, qn, offs):
    idx = unstriped(offs)
    pick = lambda x, which: x[:, which].reshape(x.shape[0], B, -1).transpose(1, 0, 2)
    k = unpack_weight(k_words, k_scales, "e4m3")
    kg = pick(k, idx)
    c = unpack_weight(c_words, c_scales, "e4m3")
    cg = pick(c, idx)
    qq = mxq(f64(qT), 1, "e4m3")
    a = (qq.transpose(0, 2, 1) @ kg) + (qq.transpose(0, 2, 1) @ cg)
    y = np.maximum(f64(qn) + pick(f64(kn), idx)[:, :1, :] - 2.0 * a, 0.0)
    return y

@@ -1,0 +1,111 @@
+from contextlib import ExitStack
+
+import concourse.mybir as mybir
+from concourse.masks import make_identity
+
+F32 = mybir.dt.float32
+BF16 = mybir.dt.bfloat16
+I32 = mybir.dt.int32
+U32 = mybir.dt.uint32
+U16 = mybir.dt.uint16
+U8 = mybir.dt.uint8
+FP8X4 = mybir.dt.float8_e4m3fn_x4
+ALU = mybir.AluOpType
+ACT = mybir.ActivationFunctionType
+
+P = 128
+T = 2048
+N = 512
+NQ = 256
+D = 512
+HALF = N // 2
+KN_ROW = 16
+FLOPS = 2 * 2 * NQ * N * D
+
+
+def tile_attend_residdist_topk_kernel(tc, qT, k_words, k_scales, c_words, c_scales, kn, qn, offs, out):
+    nc = tc.nc
+    with ExitStack() as ctx:
+        sb = ctx.enter_context(tc.tile_pool(name="sb", bufs=1))
+        ps = ctx.enter_context(tc.psum_pool(name="ps", bufs=1))
+
+        offsets = sb.tile([P, N // 16], U16, name="offsets")
+        nc.sync.dma_start(offsets[:], offs)
+
+        ks_win = sb.tile([P, T], U8, name="ks_win", align_bytes=64)
+        cs_win = sb.tile([P, T], U8, name="cs_win", align_bytes=64)
+        kn_win = sb.tile([P, T], F32, name="kn_win", align_bytes=64)
+        kw_win = sb.tile([P, T], I32, name="kw_win", align_bytes=64)
+        cw_win = sb.tile([P, T], I32, name="cw_win", align_bytes=64)
+        q_raw = sb.tile([P, 4, NQ], F32, name="q_raw", align_bytes=64)
+        qn_cols = sb.tile([P, 2], F32, name="qn_cols")
+        nc.vector.memset(ks_win[:].bitcast(I32), 0)
+        nc.vector.memset(kn_win[:].bitcast(I32), 0)
+        nc.gpsimd.memset(cs_win[:].bitcast(I32), 0)
+        for quad in range(4):
+            queue = nc.sync if quad < 2 else nc.scalar
+            queue.dma_start(ks_win[32 * quad : 32 * quad + 4, :].bitcast(I32), k_scales[0, 4 * quad : 4 * quad + 4, :].bitcast(I32))
+        nc.sync.dma_start(kw_win[:], k_words[0].rearrange("p n t -> p (n t)").bitcast(I32))
+        nc.sync.dma_start(q_raw[:], qT[0].rearrange("(p t) w -> p t w", t=4))
+        nc.sync.dma_start(kn_win[KN_ROW : KN_ROW + 1, :], kn[0:1, :])
+        for quad in range(4):
+            nc.sync.dma_start(cs_win[32 * quad + 4 : 32 * quad + 8, :].bitcast(I32), c_scales[0, 4 * quad : 4 * quad + 4, :].bitcast(I32))
+        nc.sync.dma_start(cw_win[:], c_words[0].rearrange("p n t -> p (n t)").bitcast(I32))
+        nc.sync.dma_start(qn_cols[:], qn[0].rearrange("(m j) o -> m (j o)", j=2))
+        ident = sb.tile([P, P], F32, name="ident")
+        make_identity(nc, ident[:])
+
+        ks_g = sb.tile([P, N], U8, name="ks_g", align_bytes=64)
+        cs_g = sb.tile([P, N], U8, name="cs_g", align_bytes=64)
+        kw_g = sb.tile([P, N], U32, name="kw_g", align_bytes=64)
+        kn_g = sb.tile([P, N], F32, name="kn_g", align_bytes=64)
+        nc.vector.tensor_copy(ks_g[:], ks_win[:].indirect(offsets[:]))
+        nc.vector.tensor_copy(kw_g[:], kw_win[:].bitcast(U32).indirect(offsets[:]))
+        nc.vector.tensor_copy(kn_g[:], kn_win[:].indirect(offsets[:]))
+
+        kn_t = ps.tile([P, 4, P], F32, name="kn_t")
+        for b in range(4):
+            nc.tensor.transpose(kn_t[:, b, :], kn_g[:, b * P : (b + 1) * P], ident[:])
+        kn_cols = sb.tile([P, 4], F32, name="kn_cols")
+        nc.scalar.copy(kn_cols[:], kn_t[:, :, KN_ROW])
+        kn_ps = ps.tile([P, N], F32, name="kn_ps")
+        for b in range(4):
+            nc.tensor.transpose(kn_ps[:, b * P : (b + 1) * P], kn_cols[:, b : b + 1].to_broadcast([P, P]), ident[:])
+        kn_all = sb.tile([P, N], F32, name="kn_all")
+        nc.scalar.copy(kn_all[:], kn_ps[:])
+
+        nc.vector.tensor_copy(cs_g[:], cs_win[:].indirect(offsets[:]))
+
+        q_bf = sb.tile([P, 2, P, 4], BF16, name="q_bf", tag="q_bf_then_cw", align_bytes=64)
+        nc.scalar.copy(q_bf[:], q_raw[:].rearrange("p t (m j) -> p j m t", j=2))
+        q_codes = sb.tile([P, NQ], U32, name="q_codes", align_bytes=64)
+        q_scales = sb.tile([P, NQ], U8, name="q_scales", align_bytes=64)
+        nc.vector.quantize_mx(out=q_codes[:].bitcast(FP8X4), scales=q_scales[:], in_=q_bf[:].rearrange("p j m t -> p (j m t)"))
+
+        out_v = out[0].rearrange("(m j) i -> m j i", j=2)
+        cw_g = []
+        for h in range(2):
+            g = sb.tile([P, HALF], U32, name=f"cw_g{h}", tag=("q_bf_then_cw", "cw_g1")[h], align_bytes=64)
+            nc.vector.tensor_copy(g[:], cw_win[:].bitcast(U32).indirect(offsets[:, h * 16 : (h + 1) * 16]))
+            cw_g.append(g)
+        accs = {}
+        for h in range(2):
+            cols = slice(h * HALF, (h + 1) * HALF)
+            for j in range(2):
+                rows = slice(j * P, (j + 1) * P)
+                acc = ps.tile([P, HALF], F32, name=f"acc{h}{j}")
+                accs[h, j] = acc
+                nc.tensor.matmul_mx(out=acc[:], lhsT=q_codes[:, rows].bitcast(FP8X4), lhsT_scale=q_scales[:, rows],
+                                    rhs=kw_g[:, cols].bitcast(FP8X4), rhs_scale=ks_g[:, cols], start=True, stop=False)
+        for h in range(2):
+            cols = slice(h * HALF, (h + 1) * HALF)
+            for j in range(2):
+                rows = slice(j * P, (j + 1) * P)
+                acc = accs[h, j]
+                nc.tensor.matmul_mx(out=acc[:], lhsT=q_codes[:, rows].bitcast(FP8X4), lhsT_scale=q_scales[:, rows],
+                                    rhs=cw_g[h][:].bitcast(FP8X4), rhs_scale=cs_g[4:P, cols], start=False, stop=True)
+                part = sb.tile([P, HALF], F32, name=f"part{h}{j}")
+                nc.vector.scalar_tensor_tensor(part[:], acc[:], -2.0, kn_all[:, cols], ALU.mult, ALU.add)
+                res = sb.tile([P, HALF], F32, name=f"res{h}{j}")
+                nc.scalar.activation(res[:], part[:], ACT.Relu, bias=qn_cols[:, j : j + 1])
+                nc.sync.dma_start(out_v[:, j, cols], res[:])

@@ -34,7 +34,7 @@ def tile_attend_residdist_topk_kernel(tc, qT, k_words, k_scales, c_words, c_scal
 
         ks_win = sb.tile([P, T], U8, name="ks_win", align_bytes=64)
         cs_win = sb.tile([P, T], U8, name="cs_win", align_bytes=64)
-        kn_win = sb.tile([P, T], F32, name="kn_win", align_bytes=64)
+        kn_win = sb.tile([P, T], F32, name="kn_win", tag="kn_win_then_kw_g", align_bytes=64)
         kw_win = sb.tile([P, T], I32, name="kw_win", align_bytes=64)
         cw_win = sb.tile([P, T], I32, name="cw_win", align_bytes=64)
         q_raw = sb.tile([P, 4, NQ], F32, name="q_raw", align_bytes=64)
@@ -42,26 +42,26 @@ def tile_attend_residdist_topk_kernel(tc, qT, k_words, k_scales, c_words, c_scal
         nc.vector.memset(ks_win[:].bitcast(I32), 0)
         nc.vector.memset(kn_win[:].bitcast(I32), 0)
         nc.gpsimd.memset(cs_win[:].bitcast(I32), 0)
+        nc.sync.dma_start(qn_cols[:], qn[0].rearrange("(m j) o -> m (j o)", j=2))
         for quad in range(4):
             queue = nc.sync if quad < 2 else nc.scalar
-            queue.dma_start(ks_win[32 * quad : 32 * quad + 4, :].bitcast(I32), k_scales[0, 4 * quad : 4 * quad + 4, :].bitcast(I32))
+            queue.dma_start(ks_win[quad:P:32, :].bitcast(I32), k_scales[0, quad:16:4, :].bitcast(I32))
         nc.sync.dma_start(kw_win[:], k_words[0].rearrange("p n t -> p (n t)").bitcast(I32))
         nc.sync.dma_start(q_raw[:], qT[0].rearrange("(p t) w -> p t w", t=4))
-        nc.sync.dma_start(kn_win[KN_ROW : KN_ROW + 1, :], kn[0:1, :])
+        nc.scalar.dma_start(kn_win[KN_ROW : KN_ROW + 1, :], kn[0:1, :])
         for quad in range(4):
-            nc.sync.dma_start(cs_win[32 * quad + 4 : 32 * quad + 8, :].bitcast(I32), c_scales[0, 4 * quad : 4 * quad + 4, :].bitcast(I32))
+            nc.sync.dma_start(cs_win[4 + quad : P : 32, :].bitcast(I32), c_scales[0, quad:16:4, :].bitcast(I32))
         nc.sync.dma_start(cw_win[:], c_words[0].rearrange("p n t -> p (n t)").bitcast(I32))
-        nc.sync.dma_start(qn_cols[:], qn[0].rearrange("(m j) o -> m (j o)", j=2))
         ident = sb.tile([P, P], F32, name="ident")
         make_identity(nc, ident[:])
 
         ks_g = sb.tile([P, N], U8, name="ks_g", align_bytes=64)
         cs_g = sb.tile([P, N], U8, name="cs_g", align_bytes=64)
-        kw_g = sb.tile([P, N], U32, name="kw_g", align_bytes=64)
         kn_g = sb.tile([P, N], F32, name="kn_g", align_bytes=64)
         nc.vector.tensor_copy(ks_g[:], ks_win[:].indirect(offsets[:]))
-        nc.vector.tensor_copy(kw_g[:], kw_win[:].bitcast(U32).indirect(offsets[:]))
         nc.vector.tensor_copy(kn_g[:], kn_win[:].indirect(offsets[:]))
+        kw_g = sb.tile([P, N], U32, name="kw_g", tag="kn_win_then_kw_g", align_bytes=64)
+        nc.vector.tensor_copy(kw_g[:], kw_win[:].bitcast(U32).indirect(offsets[:]))
 
         kn_t = ps.tile([P, 4, P], F32, name="kn_t")
         for b in range(4):
@@ -108,4 +108,4 @@ def tile_attend_residdist_topk_kernel(tc, qT, k_words, k_scales, c_words, c_scal
                 nc.vector.scalar_tensor_tensor(part[:], acc[:], -2.0, kn_all[:, cols], ALU.mult, ALU.add)
                 res = sb.tile([P, HALF], F32, name=f"res{h}{j}")
                 nc.scalar.activation(res[:], part[:], ACT.Relu, bias=qn_cols[:, j : j + 1])
-                nc.sync.dma_start(out_v[:, j, cols], res[:])
+                (nc.scalar if h + j == 2 else nc.sync).dma_start(out_v[:, j, cols], res[:])

@@ -34,33 +34,32 @@ def tile_attend_residdist_topk_kernel(tc, qT, k_words, k_scales, c_words, c_scal
 
         ks_win = sb.tile([P, T], U8, name="ks_win", align_bytes=64)
         cs_win = sb.tile([P, T], U8, name="cs_win", align_bytes=64)
-        kn_win = sb.tile([P, T], F32, name="kn_win", tag="kn_win_then_kw_g", align_bytes=64)
+        kn_win = sb.tile([P, T], F32, name="kn_win", tag="kn_win_then_q_codes", align_bytes=64)
         kw_win = sb.tile([P, T], I32, name="kw_win", align_bytes=64)
         cw_win = sb.tile([P, T], I32, name="cw_win", align_bytes=64)
         q_raw = sb.tile([P, 4, NQ], F32, name="q_raw", align_bytes=64)
         qn_cols = sb.tile([P, 2], F32, name="qn_cols")
         nc.vector.memset(ks_win[:].bitcast(I32), 0)
         nc.vector.memset(kn_win[:].bitcast(I32), 0)
-        nc.gpsimd.memset(cs_win[:].bitcast(I32), 0)
-        nc.sync.dma_start(qn_cols[:], qn[0].rearrange("(m j) o -> m (j o)", j=2))
-        for quad in range(4):
-            queue = nc.sync if quad < 2 else nc.scalar
-            queue.dma_start(ks_win[quad:P:32, :].bitcast(I32), k_scales[0, quad:16:4, :].bitcast(I32))
-        nc.sync.dma_start(kw_win[:], k_words[0].rearrange("p n t -> p (n t)").bitcast(I32))
+        nc.vector.memset(cs_win[:].bitcast(I32), 0)
         nc.sync.dma_start(q_raw[:], qT[0].rearrange("(p t) w -> p t w", t=4))
-        nc.scalar.dma_start(kn_win[KN_ROW : KN_ROW + 1, :], kn[0:1, :])
+        for quad in range(4):
+            nc.sync.dma_start(ks_win[quad:P:32, :].bitcast(I32), k_scales[0, quad:16:4, :].bitcast(I32))
+        nc.sync.dma_start(kn_win[KN_ROW : KN_ROW + 1, :], kn[0:1, :])
+        nc.sync.dma_start(kw_win[:], k_words[0].rearrange("p n t -> p (n t)").bitcast(I32))
         for quad in range(4):
             nc.sync.dma_start(cs_win[4 + quad : P : 32, :].bitcast(I32), c_scales[0, quad:16:4, :].bitcast(I32))
         nc.sync.dma_start(cw_win[:], c_words[0].rearrange("p n t -> p (n t)").bitcast(I32))
+        nc.sync.dma_start(qn_cols[:], qn[0].rearrange("(m j) o -> m (j o)", j=2))
         ident = sb.tile([P, P], F32, name="ident")
         make_identity(nc, ident[:])
 
         ks_g = sb.tile([P, N], U8, name="ks_g", align_bytes=64)
         cs_g = sb.tile([P, N], U8, name="cs_g", align_bytes=64)
         kn_g = sb.tile([P, N], F32, name="kn_g", align_bytes=64)
+        kw_g = sb.tile([P, N], U32, name="kw_g", align_bytes=64)
         nc.vector.tensor_copy(ks_g[:], ks_win[:].indirect(offsets[:]))
         nc.vector.tensor_copy(kn_g[:], kn_win[:].indirect(offsets[:]))
-        kw_g = sb.tile([P, N], U32, name="kw_g", tag="kn_win_then_kw_g", align_bytes=64)
         nc.vector.tensor_copy(kw_g[:], kw_win[:].bitcast(U32).indirect(offsets[:]))
 
         kn_t = ps.tile([P, 4, P], F32, name="kn_t")
@@ -76,16 +75,16 @@ def tile_attend_residdist_topk_kernel(tc, qT, k_words, k_scales, c_words, c_scal
 
         nc.vector.tensor_copy(cs_g[:], cs_win[:].indirect(offsets[:]))
 
-        q_bf = sb.tile([P, 2, P, 4], BF16, name="q_bf", tag="q_bf_then_cw", align_bytes=64)
+        q_bf = sb.tile([P, 2, P, 4], BF16, name="q_bf", align_bytes=64)
         nc.scalar.copy(q_bf[:], q_raw[:].rearrange("p t (m j) -> p j m t", j=2))
-        q_codes = sb.tile([P, NQ], U32, name="q_codes", align_bytes=64)
+        q_codes = sb.tile([P, NQ], U32, name="q_codes", tag="kn_win_then_q_codes", align_bytes=64)
         q_scales = sb.tile([P, NQ], U8, name="q_scales", align_bytes=64)
         nc.vector.quantize_mx(out=q_codes[:].bitcast(FP8X4), scales=q_scales[:], in_=q_bf[:].rearrange("p j m t -> p (j m t)"))
 
         out_v = out[0].rearrange("(m j) i -> m j i", j=2)
         cw_g = []
         for h in range(2):
-            g = sb.tile([P, HALF], U32, name=f"cw_g{h}", tag=("q_bf_then_cw", "cw_g1")[h], align_bytes=64)
+            g = sb.tile([P, HALF], U32, name=f"cw_g{h}", align_bytes=64)
             nc.vector.tensor_copy(g[:], cw_win[:].bitcast(U32).indirect(offsets[:, h * 16 : (h + 1) * 16]))
             cw_g.append(g)
         accs = {}

@@ -42,9 +42,11 @@ def tile_attend_residdist_topk_kernel(tc, qT, k_words, k_scales, c_words, c_scal
         nc.vector.memset(ks_win[:].bitcast(I32), 0)
         nc.vector.memset(kn_win[:].bitcast(I32), 0)
         nc.vector.memset(cs_win[:].bitcast(I32), 0)
-        nc.sync.dma_start(q_raw[:], qT[0].rearrange("(p t) w -> p t w", t=4))
+        q_rows = qT[0].rearrange("(p t) w -> p t w", t=4)
+        nc.sync.dma_start(q_raw[:, 0:2, :], q_rows[:, 0:2, :])
         for quad in range(4):
             nc.sync.dma_start(ks_win[quad:P:32, :].bitcast(I32), k_scales[0, quad:16:4, :].bitcast(I32))
+        nc.sync.dma_start(q_raw[:, 2:4, :], q_rows[:, 2:4, :])
         nc.sync.dma_start(kn_win[KN_ROW : KN_ROW + 1, :], kn[0:1, :])
         nc.sync.dma_start(kw_win[:], k_words[0].rearrange("p n t -> p (n t)").bitcast(I32))
         for quad in range(4):
@@ -76,7 +78,8 @@ def tile_attend_residdist_topk_kernel(tc, qT, k_words, k_scales, c_words, c_scal
         nc.vector.tensor_copy(cs_g[:], cs_win[:].indirect(offsets[:]))
 
         q_bf = sb.tile([P, 2, P, 4], BF16, name="q_bf", align_bytes=64)
-        nc.scalar.copy(q_bf[:], q_raw[:].rearrange("p t (m j) -> p j m t", j=2))
+        for t0 in (0, 2):
+            nc.scalar.copy(q_bf[:, :, :, t0 : t0 + 2], q_raw[:, t0 : t0 + 2, :].rearrange("p t (m j) -> p j m t", j=2))
         q_codes = sb.tile([P, NQ], U32, name="q_codes", tag="kn_win_then_q_codes", align_bytes=64)
         q_scales = sb.tile([P, NQ], U8, name="q_scales", align_bytes=64)
         nc.vector.quantize_mx(out=q_codes[:].bitcast(FP8X4), scales=q_scales[:], in_=q_bf[:].rearrange("p j m t -> p (j m t)"))

@@ -1,7 +1,6 @@
 from contextlib import ExitStack
 
 import concourse.mybir as mybir
-from concourse.masks import make_identity
 
 F32 = mybir.dt.float32
 BF16 = mybir.dt.bfloat16
@@ -34,35 +33,45 @@ def tile_attend_residdist_topk_kernel(tc, qT, k_words, k_scales, c_words, c_scal
 
         ks_win = sb.tile([P, T], U8, name="ks_win", align_bytes=64)
         cs_win = sb.tile([P, T], U8, name="cs_win", align_bytes=64)
-        kn_win = sb.tile([P, T], F32, name="kn_win", tag="kn_win_then_q_codes", align_bytes=64)
-        kw_win = sb.tile([P, T], I32, name="kw_win", align_bytes=64)
+        kn_win = sb.tile([P, T], F32, name="kn_win", tag="kn_win_then_kw_g", align_bytes=64)
+        kw_win = sb.tile([P, T], I32, name="kw_win", tag="kw_win_then_q_codes", align_bytes=64)
         cw_win = sb.tile([P, T], I32, name="cw_win", align_bytes=64)
         q_raw = sb.tile([P, 4, NQ], F32, name="q_raw", align_bytes=64)
         qn_cols = sb.tile([P, 2], F32, name="qn_cols")
+        planes = sb.tile([P, 2, N], U8, name="planes", align_bytes=64)
+        ident = sb.tile([P, P], F32, name="ident")
         nc.vector.memset(ks_win[:].bitcast(I32), 0)
-        nc.vector.memset(kn_win[:].bitcast(I32), 0)
         nc.vector.memset(cs_win[:].bitcast(I32), 0)
+        nc.vector.memset(kn_win[:].bitcast(I32), 0)
+        nc.vector.memset(planes[:].rearrange("p a n -> p (a n)").bitcast(I32), 0)
+        nc.vector.memset(ident[:], 0.0)
+        nc.gpsimd.affine_select(out=ident[:], in_=ident[:], compare_op=ALU.not_equal, fill=1.0, base=0,
+                                pattern=[[-1, P]], channel_multiplier=1)
         q_rows = qT[0].rearrange("(p t) w -> p t w", t=4)
         nc.sync.dma_start(q_raw[:, 0:2, :], q_rows[:, 0:2, :])
-        for quad in range(4):
-            nc.sync.dma_start(ks_win[quad:P:32, :].bitcast(I32), k_scales[0, quad:16:4, :].bitcast(I32))
-        nc.sync.dma_start(q_raw[:, 2:4, :], q_rows[:, 2:4, :])
-        nc.sync.dma_start(kn_win[KN_ROW : KN_ROW + 1, :], kn[0:1, :])
+        nc.sync.dma_start(ks_win[0:P:8, :].bitcast(I32), k_scales[0].bitcast(I32))
+        nc.sync.dma_start(cs_win[4:P:8, :].bitcast(I32), c_scales[0].bitcast(I32))
         nc.sync.dma_start(kw_win[:], k_words[0].rearrange("p n t -> p (n t)").bitcast(I32))
-        for quad in range(4):
-            nc.sync.dma_start(cs_win[4 + quad : P : 32, :].bitcast(I32), c_scales[0, quad:16:4, :].bitcast(I32))
+        nc.sync.dma_start(kn_win[KN_ROW : KN_ROW + 1, :], kn[0:1, :])
+        nc.sync.dma_start(q_raw[:, 2:4, :], q_rows[:, 2:4, :])
         nc.sync.dma_start(cw_win[:], c_words[0].rearrange("p n t -> p (n t)").bitcast(I32))
         nc.sync.dma_start(qn_cols[:], qn[0].rearrange("(m j) o -> m (j o)", j=2))
-        ident = sb.tile([P, P], F32, name="ident")
-        make_identity(nc, ident[:])
 
+        q_bf = sb.tile([P, 2, P, 4], BF16, name="q_bf", align_bytes=64)
+        nc.scalar.copy(q_bf[:, :, :, 0:2], q_raw[:, 0:2, :].rearrange("p t (m j) -> p j m t", j=2))
         ks_g = sb.tile([P, N], U8, name="ks_g", align_bytes=64)
         cs_g = sb.tile([P, N], U8, name="cs_g", align_bytes=64)
         kn_g = sb.tile([P, N], F32, name="kn_g", align_bytes=64)
-        kw_g = sb.tile([P, N], U32, name="kw_g", align_bytes=64)
         nc.vector.tensor_copy(ks_g[:], ks_win[:].indirect(offsets[:]))
+        for r in range(4):
+            nc.scalar.dma_start(planes[r:P:32, 0, :].bitcast(I32), ks_g[8 * r : P : 32, :].bitcast(I32))
+        nc.vector.tensor_copy(cs_g[:], cs_win[:].indirect(offsets[:]))
+        for r in range(4):
+            nc.scalar.dma_start(planes[r:P:32, 1, :].bitcast(I32), cs_g[8 * r + 4 : P : 32, :].bitcast(I32))
         nc.vector.tensor_copy(kn_g[:], kn_win[:].indirect(offsets[:]))
+        kw_g = sb.tile([P, N], U32, name="kw_g", tag="kn_win_then_kw_g", align_bytes=64)
         nc.vector.tensor_copy(kw_g[:], kw_win[:].bitcast(U32).indirect(offsets[:]))
+        nc.scalar.copy(q_bf[:, :, :, 2:4], q_raw[:, 2:4, :].rearrange("p t (m j) -> p j m t", j=2))
 
         kn_t = ps.tile([P, 4, P], F32, name="kn_t")
         for b in range(4):
@@ -75,12 +84,7 @@ def tile_attend_residdist_topk_kernel(tc, qT, k_words, k_scales, c_words, c_scal
         kn_all = sb.tile([P, N], F32, name="kn_all")
         nc.scalar.copy(kn_all[:], kn_ps[:])
 
-        nc.vector.tensor_copy(cs_g[:], cs_win[:].indirect(offsets[:]))
-
-        q_bf = sb.tile([P, 2, P, 4], BF16, name="q_bf", align_bytes=64)
-        for t0 in (0, 2):
-            nc.scalar.copy(q_bf[:, :, :, t0 : t0 + 2], q_raw[:, t0 : t0 + 2, :].rearrange("p t (m j) -> p j m t", j=2))
-        q_codes = sb.tile([P, NQ], U32, name="q_codes", tag="kn_win_then_q_codes", align_bytes=64)
+        q_codes = sb.tile([P, NQ], U32, name="q_codes", tag="kw_win_then_q_codes", align_bytes=64)
         q_scales = sb.tile([P, NQ], U8, name="q_scales", align_bytes=64)
         nc.vector.quantize_mx(out=q_codes[:].bitcast(FP8X4), scales=q_scales[:], in_=q_bf[:].rearrange("p j m t -> p (j m t)"))
 
@@ -98,14 +102,14 @@ def tile_attend_residdist_topk_kernel(tc, qT, k_words, k_scales, c_words, c_scal
                 acc = ps.tile([P, HALF], F32, name=f"acc{h}{j}")
                 accs[h, j] = acc
                 nc.tensor.matmul_mx(out=acc[:], lhsT=q_codes[:, rows].bitcast(FP8X4), lhsT_scale=q_scales[:, rows],
-                                    rhs=kw_g[:, cols].bitcast(FP8X4), rhs_scale=ks_g[:, cols], start=True, stop=False)
+                                    rhs=kw_g[:, cols].bitcast(FP8X4), rhs_scale=planes[:, 0, cols], start=True, stop=False)
         for h in range(2):
             cols = slice(h * HALF, (h + 1) * HALF)
             for j in range(2):
                 rows = slice(j * P, (j + 1) * P)
                 acc = accs[h, j]
                 nc.tensor.matmul_mx(out=acc[:], lhsT=q_codes[:, rows].bitcast(FP8X4), lhsT_scale=q_scales[:, rows],
-                                    rhs=cw_g[h][:].bitcast(FP8X4), rhs_scale=cs_g[4:P, cols], start=False, stop=True)
+                                    rhs=cw_g[h][:].bitcast(FP8X4), rhs_scale=planes[:, 1, cols], start=False, stop=True)
                 part = sb.tile([P, HALF], F32, name=f"part{h}{j}")
                 nc.vector.scalar_tensor_tensor(part[:], acc[:], -2.0, kn_all[:, cols], ALU.mult, ALU.add)
                 res = sb.tile([P, HALF], F32, name=f"res{h}{j}")

@@ -18,8 +18,9 @@ N = 512
 NQ = 256
 D = 512
 HALF = N // 2
-KN_ROW = 16
 FLOPS = 2 * 2 * NQ * N * D
+CW_FIRST = 768
+KN_COLS = T // P
 
 
 def tile_attend_residdist_topk_kernel(tc, qT, k_words, k_scales, c_words, c_scales, kn, qn, offs, out):
@@ -29,64 +30,65 @@ def tile_attend_residdist_topk_kernel(tc, qT, k_words, k_scales, c_words, c_scal
         ps = ctx.enter_context(tc.psum_pool(name="ps", bufs=1))
 
         offsets = sb.tile([P, N // 16], U16, name="offsets")
-        nc.sync.dma_start(offsets[:], offs)
-
         ks_win = sb.tile([P, T], U8, name="ks_win", align_bytes=64)
         cs_win = sb.tile([P, T], U8, name="cs_win", align_bytes=64)
-        kn_win = sb.tile([P, T], F32, name="kn_win", tag="kn_win_then_kw_g", align_bytes=64)
-        kw_win = sb.tile([P, T], I32, name="kw_win", tag="kw_win_then_q_codes", align_bytes=64)
+        kn_win = sb.tile([P, T], F32, name="kn_win", align_bytes=64)
+        kw_win = sb.tile([P, T], I32, name="kw_win", tag="kw_win_then_kn_g", align_bytes=64)
         cw_win = sb.tile([P, T], I32, name="cw_win", align_bytes=64)
         q_raw = sb.tile([P, 4, NQ], F32, name="q_raw", align_bytes=64)
         qn_cols = sb.tile([P, 2], F32, name="qn_cols")
-        planes = sb.tile([P, 2, N], U8, name="planes", align_bytes=64)
+        kn_cols = sb.tile([P, KN_COLS], F32, name="kn_cols")
+        k_plane = sb.tile([P, N], U8, name="k_plane", align_bytes=64)
+        c_plane = sb.tile([P, N], U8, name="c_plane", align_bytes=64)
         ident = sb.tile([P, P], F32, name="ident")
         nc.vector.memset(ks_win[:].bitcast(I32), 0)
         nc.vector.memset(cs_win[:].bitcast(I32), 0)
-        nc.vector.memset(kn_win[:].bitcast(I32), 0)
-        nc.vector.memset(planes[:].rearrange("p a n -> p (a n)").bitcast(I32), 0)
         nc.vector.memset(ident[:], 0.0)
+        nc.vector.memset(k_plane[:].bitcast(I32), 0)
+        nc.vector.memset(c_plane[:].bitcast(I32), 0)
         nc.gpsimd.affine_select(out=ident[:], in_=ident[:], compare_op=ALU.not_equal, fill=1.0, base=0,
                                 pattern=[[-1, P]], channel_multiplier=1)
         q_rows = qT[0].rearrange("(p t) w -> p t w", t=4)
+        cw_rows = c_words[0].rearrange("p n t -> p (n t)").bitcast(I32)
         nc.sync.dma_start(q_raw[:, 0:2, :], q_rows[:, 0:2, :])
+        nc.scalar.dma_start(qn_cols[:], qn[0].rearrange("(m j) o -> m (j o)", j=2))
+        nc.sync.dma_start(offsets[:], offs)
         nc.sync.dma_start(ks_win[0:P:8, :].bitcast(I32), k_scales[0].bitcast(I32))
+        nc.sync.dma_start(q_raw[:, 2:4, :], q_rows[:, 2:4, :])
+        nc.sync.dma_start(kn_cols[:], kn[0].rearrange("(p c) -> p c", c=KN_COLS))
         nc.sync.dma_start(cs_win[4:P:8, :].bitcast(I32), c_scales[0].bitcast(I32))
         nc.sync.dma_start(kw_win[:], k_words[0].rearrange("p n t -> p (n t)").bitcast(I32))
-        nc.sync.dma_start(kn_win[KN_ROW : KN_ROW + 1, :], kn[0:1, :])
-        nc.sync.dma_start(q_raw[:, 2:4, :], q_rows[:, 2:4, :])
-        nc.sync.dma_start(cw_win[:], c_words[0].rearrange("p n t -> p (n t)").bitcast(I32))
-        nc.sync.dma_start(qn_cols[:], qn[0].rearrange("(m j) o -> m (j o)", j=2))
+        nc.sync.dma_start(cw_win[:, :CW_FIRST], cw_rows[:, :CW_FIRST])
 
-        q_bf = sb.tile([P, 2, P, 4], BF16, name="q_bf", align_bytes=64)
-        nc.scalar.copy(q_bf[:, :, :, 0:2], q_raw[:, 0:2, :].rearrange("p t (m j) -> p j m t", j=2))
         ks_g = sb.tile([P, N], U8, name="ks_g", align_bytes=64)
         cs_g = sb.tile([P, N], U8, name="cs_g", align_bytes=64)
-        kn_g = sb.tile([P, N], F32, name="kn_g", align_bytes=64)
         nc.vector.tensor_copy(ks_g[:], ks_win[:].indirect(offsets[:]))
         for r in range(4):
-            nc.scalar.dma_start(planes[r:P:32, 0, :].bitcast(I32), ks_g[8 * r : P : 32, :].bitcast(I32))
+            nc.sync.dma_start(k_plane[r:P:32, :].bitcast(I32), ks_g[8 * r : P : 32, :].bitcast(I32))
+        nc.sync.dma_start(cw_win[:, CW_FIRST:], cw_rows[:, CW_FIRST:])
         nc.vector.tensor_copy(cs_g[:], cs_win[:].indirect(offsets[:]))
         for r in range(4):
-            nc.scalar.dma_start(planes[r:P:32, 1, :].bitcast(I32), cs_g[8 * r + 4 : P : 32, :].bitcast(I32))
-        nc.vector.tensor_copy(kn_g[:], kn_win[:].indirect(offsets[:]))
-        kw_g = sb.tile([P, N], U32, name="kw_g", tag="kn_win_then_kw_g", align_bytes=64)
-        nc.vector.tensor_copy(kw_g[:], kw_win[:].bitcast(U32).indirect(offsets[:]))
-        nc.scalar.copy(q_bf[:, :, :, 2:4], q_raw[:, 2:4, :].rearrange("p t (m j) -> p j m t", j=2))
+            nc.sync.dma_start(c_plane[r:P:32, :].bitcast(I32), cs_g[8 * r + 4 : P : 32, :].bitcast(I32))
 
-        kn_t = ps.tile([P, 4, P], F32, name="kn_t")
-        for b in range(4):
-            nc.tensor.transpose(kn_t[:, b, :], kn_g[:, b * P : (b + 1) * P], ident[:])
-        kn_cols = sb.tile([P, 4], F32, name="kn_cols")
-        nc.scalar.copy(kn_cols[:], kn_t[:, :, KN_ROW])
-        kn_ps = ps.tile([P, N], F32, name="kn_ps")
-        for b in range(4):
-            nc.tensor.transpose(kn_ps[:, b * P : (b + 1) * P], kn_cols[:, b : b + 1].to_broadcast([P, P]), ident[:])
-        kn_all = sb.tile([P, N], F32, name="kn_all")
-        nc.scalar.copy(kn_all[:], kn_ps[:])
-
-        q_codes = sb.tile([P, NQ], U32, name="q_codes", tag="kw_win_then_q_codes", align_bytes=64)
+        q_bf = sb.tile([P, 2, P, 4], BF16, name="q_bf", align_bytes=64)
+        for t0 in (0, 2):
+            nc.scalar.copy(q_bf[:, :, :, t0 : t0 + 2], q_raw[:, t0 : t0 + 2, :].rearrange("p t (m j) -> p j m t", j=2))
+        q_codes = sb.tile([P, NQ], U32, name="q_codes", align_bytes=64)
         q_scales = sb.tile([P, NQ], U8, name="q_scales", align_bytes=64)
         nc.vector.quantize_mx(out=q_codes[:].bitcast(FP8X4), scales=q_scales[:], in_=q_bf[:].rearrange("p j m t -> p (j m t)"))
+
+        kn_by_col = kn_win[:].rearrange("m (p c) -> m p c", c=KN_COLS)
+        for b in range(4):
+            bank = ps.tile([P, 4, P], F32, name=f"kn_bank{b}")
+            for e in range(4):
+                c = 4 * b + e
+                nc.tensor.transpose(bank[:, e, :], kn_cols[:, c : c + 1].to_broadcast([P, P]), ident[:])
+            nc.scalar.copy(kn_by_col[:, :, 4 * b : 4 * b + 4], bank[:].rearrange("m e p -> m p e"))
+
+        kw_g = sb.tile([P, N], U32, name="kw_g", align_bytes=64)
+        nc.vector.tensor_copy(kw_g[:], kw_win[:].bitcast(U32).indirect(offsets[:]))
+        kn_g = sb.tile([P, N], F32, name="kn_g", tag="kw_win_then_kn_g", align_bytes=64)
+        nc.vector.tensor_copy(kn_g[:], kn_win[:].indirect(offsets[:]))
 
         out_v = out[0].rearrange("(m j) i -> m j i", j=2)
         cw_g = []
@@ -102,16 +104,16 @@ def tile_attend_residdist_topk_kernel(tc, qT, k_words, k_scales, c_words, c_scal
                 acc = ps.tile([P, HALF], F32, name=f"acc{h}{j}")
                 accs[h, j] = acc
                 nc.tensor.matmul_mx(out=acc[:], lhsT=q_codes[:, rows].bitcast(FP8X4), lhsT_scale=q_scales[:, rows],
-                                    rhs=kw_g[:, cols].bitcast(FP8X4), rhs_scale=planes[:, 0, cols], start=True, stop=False)
+                                    rhs=kw_g[:, cols].bitcast(FP8X4), rhs_scale=k_plane[:, cols], start=True, stop=False)
         for h in range(2):
             cols = slice(h * HALF, (h + 1) * HALF)
             for j in range(2):
                 rows = slice(j * P, (j + 1) * P)
                 acc = accs[h, j]
                 nc.tensor.matmul_mx(out=acc[:], lhsT=q_codes[:, rows].bitcast(FP8X4), lhsT_scale=q_scales[:, rows],
-                                    rhs=cw_g[h][:].bitcast(FP8X4), rhs_scale=planes[:, 1, cols], start=False, stop=True)
+                                    rhs=cw_g[h][:].bitcast(FP8X4), rhs_scale=c_plane[:, cols], start=False, stop=True)
                 part = sb.tile([P, HALF], F32, name=f"part{h}{j}")
-                nc.vector.scalar_tensor_tensor(part[:], acc[:], -2.0, kn_all[:, cols], ALU.mult, ALU.add)
+                nc.vector.scalar_tensor_tensor(part[:], acc[:], -2.0, kn_g[:, cols], ALU.mult, ALU.add)
                 res = sb.tile([P, HALF], F32, name=f"res{h}{j}")
                 nc.scalar.activation(res[:], part[:], ACT.Relu, bias=qn_cols[:, j : j + 1])
                 (nc.scalar if h + j == 2 else nc.sync).dma_start(out_v[:, j, cols], res[:])

@@ -32,10 +32,9 @@ def tile_attend_residdist_topk_kernel(tc, qT, k_words, k_scales, c_words, c_scal
         offsets = sb.tile([P, N // 16], U16, name="offsets")
         ks_win = sb.tile([P, T], U8, name="ks_win", align_bytes=64)
         cs_win = sb.tile([P, T], U8, name="cs_win", align_bytes=64)
-        kn_win = sb.tile([P, T], F32, name="kn_win", align_bytes=64)
         kw_win = sb.tile([P, T], I32, name="kw_win", tag="kw_win_then_kn_g", align_bytes=64)
         cw_win = sb.tile([P, T], I32, name="cw_win", align_bytes=64)
-        q_raw = sb.tile([P, 4, NQ], F32, name="q_raw", align_bytes=64)
+        q_raw = sb.tile([P, 4, NQ], F32, name="q_raw", tag="q_raw_then_kn_win", align_bytes=64)
         qn_cols = sb.tile([P, 2], F32, name="qn_cols")
         kn_cols = sb.tile([P, KN_COLS], F32, name="kn_cols")
         k_plane = sb.tile([P, N], U8, name="k_plane", align_bytes=64)
@@ -51,14 +50,14 @@ def tile_attend_residdist_topk_kernel(tc, qT, k_words, k_scales, c_words, c_scal
         q_rows = qT[0].rearrange("(p t) w -> p t w", t=4)
         cw_rows = c_words[0].rearrange("p n t -> p (n t)").bitcast(I32)
         nc.sync.dma_start(q_raw[:, 0:2, :], q_rows[:, 0:2, :])
-        nc.scalar.dma_start(qn_cols[:], qn[0].rearrange("(m j) o -> m (j o)", j=2))
+        nc.scalar.dma_start(kn_cols[:], kn[0].rearrange("(p c) -> p c", c=KN_COLS))
         nc.sync.dma_start(offsets[:], offs)
         nc.sync.dma_start(ks_win[0:P:8, :].bitcast(I32), k_scales[0].bitcast(I32))
         nc.sync.dma_start(q_raw[:, 2:4, :], q_rows[:, 2:4, :])
-        nc.sync.dma_start(kn_cols[:], kn[0].rearrange("(p c) -> p c", c=KN_COLS))
         nc.sync.dma_start(cs_win[4:P:8, :].bitcast(I32), c_scales[0].bitcast(I32))
         nc.sync.dma_start(kw_win[:], k_words[0].rearrange("p n t -> p (n t)").bitcast(I32))
         nc.sync.dma_start(cw_win[:, :CW_FIRST], cw_rows[:, :CW_FIRST])
+        nc.sync.dma_start(qn_cols[:], qn[0].rearrange("(m j) o -> m (j o)", j=2))
 
         ks_g = sb.tile([P, N], U8, name="ks_g", align_bytes=64)
         cs_g = sb.tile([P, N], U8, name="cs_g", align_bytes=64)
@@ -77,6 +76,7 @@ def tile_attend_residdist_topk_kernel(tc, qT, k_words, k_scales, c_words, c_scal
         q_scales = sb.tile([P, NQ], U8, name="q_scales", align_bytes=64)
         nc.vector.quantize_mx(out=q_codes[:].bitcast(FP8X4), scales=q_scales[:], in_=q_bf[:].rearrange("p j m t -> p (j m t)"))
 
+        kn_win = sb.tile([P, T], F32, name="kn_win", tag="q_raw_then_kn_win", align_bytes=64)
         kn_by_col = kn_win[:].rearrange("m (p c) -> m p c", c=KN_COLS)
         for b in range(4):
             bank = ps.tile([P, 4, P], F32, name=f"kn_bank{b}")

@@ -19,7 +19,7 @@ NQ = 256
 D = 512
 HALF = N // 2
 FLOPS = 2 * 2 * NQ * N * D
-CW_FIRST = 768
+CW_FIRST = 1024
 KN_COLS = T // P
 
 
@@ -32,7 +32,7 @@ def tile_attend_residdist_topk_kernel(tc, qT, k_words, k_scales, c_words, c_scal
         offsets = sb.tile([P, N // 16], U16, name="offsets")
         ks_win = sb.tile([P, T], U8, name="ks_win", align_bytes=64)
         cs_win = sb.tile([P, T], U8, name="cs_win", align_bytes=64)
-        kw_win = sb.tile([P, T], I32, name="kw_win", tag="kw_win_then_kn_g", align_bytes=64)
+        kw_win = sb.tile([P, T], I32, name="kw_win", align_bytes=64)
         cw_win = sb.tile([P, T], I32, name="cw_win", align_bytes=64)
         q_raw = sb.tile([P, 4, NQ], F32, name="q_raw", tag="q_raw_then_kn_win", align_bytes=64)
         qn_cols = sb.tile([P, 2], F32, name="qn_cols")
@@ -87,7 +87,7 @@ def tile_attend_residdist_topk_kernel(tc, qT, k_words, k_scales, c_words, c_scal
 
         kw_g = sb.tile([P, N], U32, name="kw_g", align_bytes=64)
         nc.vector.tensor_copy(kw_g[:], kw_win[:].bitcast(U32).indirect(offsets[:]))
-        kn_g = sb.tile([P, N], F32, name="kn_g", tag="kw_win_then_kn_g", align_bytes=64)
+        kn_g = sb.tile([P, N], F32, name="kn_g", align_bytes=64)
         nc.vector.tensor_copy(kn_g[:], kn_win[:].indirect(offsets[:]))
 
         out_v = out[0].rearrange("(m j) i -> m j i", j=2)

@@ -19,7 +19,7 @@ NQ = 256
 D = 512
 HALF = N // 2
 FLOPS = 2 * 2 * NQ * N * D
-CW_FIRST = 1024
+CW_FIRST = 896
 KN_COLS = T // P
 
 
@@ -51,13 +51,13 @@ def tile_attend_residdist_topk_kernel(tc, qT, k_words, k_scales, c_words, c_scal
         cw_rows = c_words[0].rearrange("p n t -> p (n t)").bitcast(I32)
         nc.sync.dma_start(q_raw[:, 0:2, :], q_rows[:, 0:2, :])
         nc.scalar.dma_start(kn_cols[:], kn[0].rearrange("(p c) -> p c", c=KN_COLS))
+        nc.scalar.dma_start(qn_cols[:], qn[0].rearrange("(m j) o -> m (j o)", j=2))
         nc.sync.dma_start(offsets[:], offs)
         nc.sync.dma_start(ks_win[0:P:8, :].bitcast(I32), k_scales[0].bitcast(I32))
         nc.sync.dma_start(q_raw[:, 2:4, :], q_rows[:, 2:4, :])
         nc.sync.dma_start(cs_win[4:P:8, :].bitcast(I32), c_scales[0].bitcast(I32))
         nc.sync.dma_start(kw_win[:], k_words[0].rearrange("p n t -> p (n t)").bitcast(I32))
         nc.sync.dma_start(cw_win[:, :CW_FIRST], cw_rows[:, :CW_FIRST])
-        nc.sync.dma_start(qn_cols[:], qn[0].rearrange("(m j) o -> m (j o)", j=2))
 
         ks_g = sb.tile([P, N], U8, name="ks_g", align_bytes=64)
         cs_g = sb.tile([P, N], U8, name="cs_g", align_bytes=64)

@@ -51,7 +51,6 @@ def tile_attend_residdist_topk_kernel(tc, qT, k_words, k_scales, c_words, c_scal
         cw_rows = c_words[0].rearrange("p n t -> p (n t)").bitcast(I32)
         nc.sync.dma_start(q_raw[:, 0:2, :], q_rows[:, 0:2, :])
         nc.scalar.dma_start(kn_cols[:], kn[0].rearrange("(p c) -> p c", c=KN_COLS))
-        nc.scalar.dma_start(qn_cols[:], qn[0].rearrange("(m j) o -> m (j o)", j=2))
         nc.sync.dma_start(offsets[:], offs)
         nc.sync.dma_start(ks_win[0:P:8, :].bitcast(I32), k_scales[0].bitcast(I32))
         nc.sync.dma_start(q_raw[:, 2:4, :], q_rows[:, 2:4, :])
@@ -68,6 +67,7 @@ def tile_attend_residdist_topk_kernel(tc, qT, k_words, k_scales, c_words, c_scal
         nc.vector.tensor_copy(cs_g[:], cs_win[:].indirect(offsets[:]))
         for r in range(4):
             nc.sync.dma_start(c_plane[r:P:32, :].bitcast(I32), cs_g[8 * r + 4 : P : 32, :].bitcast(I32))
+        nc.sync.dma_start(qn_cols[:], qn[0].rearrange("(m j) o -> m (j o)", j=2))
 
         q_bf = sb.tile([P, 2, P, 4], BF16, name="q_bf", align_bytes=64)
         for t0 in (0, 2):

@@ -34,7 +34,8 @@ def tile_attend_residdist_topk_kernel(tc, qT, k_words, k_scales, c_words, c_scal
         cs_win = sb.tile([P, T], U8, name="cs_win", align_bytes=64)
         kw_win = sb.tile([P, T], I32, name="kw_win", align_bytes=64)
         cw_win = sb.tile([P, T], I32, name="cw_win", align_bytes=64)
-        q_raw = sb.tile([P, 4, NQ], F32, name="q_raw", tag="q_raw_then_kn_win", align_bytes=64)
+        q_raw0 = sb.tile([P, 2, NQ], F32, name="q_raw0", tag="q_raw_then_kn_win", align_bytes=64)
+        q_raw1 = sb.tile([P, 2, NQ], F32, name="q_raw1", align_bytes=64)
         qn_cols = sb.tile([P, 2], F32, name="qn_cols")
         kn_cols = sb.tile([P, KN_COLS], F32, name="kn_cols")
         k_plane = sb.tile([P, N], U8, name="k_plane", align_bytes=64)
@@ -49,11 +50,11 @@ def tile_attend_residdist_topk_kernel(tc, qT, k_words, k_scales, c_words, c_scal
                                 pattern=[[-1, P]], channel_multiplier=1)
         q_rows = qT[0].rearrange("(p t) w -> p t w", t=4)
         cw_rows = c_words[0].rearrange("p n t -> p (n t)").bitcast(I32)
-        nc.sync.dma_start(q_raw[:, 0:2, :], q_rows[:, 0:2, :])
+        nc.sync.dma_start(q_raw0[:], q_rows[:, 0:2, :])
         nc.scalar.dma_start(kn_cols[:], kn[0].rearrange("(p c) -> p c", c=KN_COLS))
         nc.sync.dma_start(offsets[:], offs)
         nc.sync.dma_start(ks_win[0:P:8, :].bitcast(I32), k_scales[0].bitcast(I32))
-        nc.sync.dma_start(q_raw[:, 2:4, :], q_rows[:, 2:4, :])
+        nc.sync.dma_start(q_raw1[:], q_rows[:, 2:4, :])
         nc.sync.dma_start(cs_win[4:P:8, :].bitcast(I32), c_scales[0].bitcast(I32))
         nc.sync.dma_start(kw_win[:], k_words[0].rearrange("p n t -> p (n t)").bitcast(I32))
         nc.sync.dma_start(cw_win[:, :CW_FIRST], cw_rows[:, :CW_FIRST])
@@ -70,8 +71,8 @@ def tile_attend_residdist_topk_kernel(tc, qT, k_words, k_scales, c_words, c_scal
         nc.sync.dma_start(qn_cols[:], qn[0].rearrange("(m j) o -> m (j o)", j=2))
 
         q_bf = sb.tile([P, 2, P, 4], BF16, name="q_bf", align_bytes=64)
-        for t0 in (0, 2):
-            nc.scalar.copy(q_bf[:, :, :, t0 : t0 + 2], q_raw[:, t0 : t0 + 2, :].rearrange("p t (m j) -> p j m t", j=2))
+        for t0, q_raw in ((0, q_raw0), (2, q_raw1)):
+            nc.scalar.copy(q_bf[:, :, :, t0 : t0 + 2], q_raw[:].rearrange("p t (m j) -> p j m t", j=2))
         q_codes = sb.tile([P, NQ], U32, name="q_codes", align_bytes=64)
         q_scales = sb.tile([P, NQ], U8, name="q_scales", align_bytes=64)
         nc.vector.quantize_mx(out=q_codes[:].bitcast(FP8X4), scales=q_scales[:], in_=q_bf[:].rearrange("p j m t -> p (j m t)"))

@@ -80,7 +80,7 @@ def tile_attend_residdist_topk_kernel(tc, qT, k_words, k_scales, c_words, c_scal
         kn_win = sb.tile([P, T], F32, name="kn_win", tag="q_raw_then_kn_win", align_bytes=64)
         kn_by_col = kn_win[:].rearrange("m (p c) -> m p c", c=KN_COLS)
         for b in range(4):
-            bank = ps.tile([P, 4, P], F32, name=f"kn_bank{b}")
+            bank = ps.tile([P, 4, P], F32, name=f"kn_bank{b}", tag=f"bank{b}")
             for e in range(4):
                 c = 4 * b + e
                 nc.tensor.transpose(bank[:, e, :], kn_cols[:, c : c + 1].to_broadcast([P, P]), ident[:])
@@ -97,24 +97,27 @@ def tile_attend_residdist_topk_kernel(tc, qT, k_words, k_scales, c_words, c_scal
             g = sb.tile([P, HALF], U32, name=f"cw_g{h}", align_bytes=64)
             nc.vector.tensor_copy(g[:], cw_win[:].bitcast(U32).indirect(offsets[:, h * 16 : (h + 1) * 16]))
             cw_g.append(g)
+        QUARTER = N // 4
+        pieces = [(h, j, e) for h in range(2) for j in range(2) for e in range(2)]
         accs = {}
+        for n, (h, j, e) in enumerate(pieces):
+            cols = slice((2 * h + e) * QUARTER, (2 * h + e + 1) * QUARTER)
+            rows = slice(j * P, (j + 1) * P)
+            acc = ps.tile([P, QUARTER], F32, name=f"acc{n}", tag=f"bank{(n + 4) % 8}")
+            accs[h, j, e] = acc
+            nc.tensor.matmul_mx(out=acc[:], lhsT=q_codes[:, rows].bitcast(FP8X4), lhsT_scale=q_scales[:, rows],
+                                rhs=kw_g[:, cols].bitcast(FP8X4), rhs_scale=k_plane[:, cols], start=True, stop=False)
         for h in range(2):
-            cols = slice(h * HALF, (h + 1) * HALF)
             for j in range(2):
                 rows = slice(j * P, (j + 1) * P)
-                acc = ps.tile([P, HALF], F32, name=f"acc{h}{j}")
-                accs[h, j] = acc
-                nc.tensor.matmul_mx(out=acc[:], lhsT=q_codes[:, rows].bitcast(FP8X4), lhsT_scale=q_scales[:, rows],
-                                    rhs=kw_g[:, cols].bitcast(FP8X4), rhs_scale=k_plane[:, cols], start=True, stop=False)
-        for h in range(2):
-            cols = slice(h * HALF, (h + 1) * HALF)
-            for j in range(2):
-                rows = slice(j * P, (j + 1) * P)
-                acc = accs[h, j]
-                nc.tensor.matmul_mx(out=acc[:], lhsT=q_codes[:, rows].bitcast(FP8X4), lhsT_scale=q_scales[:, rows],
-                                    rhs=cw_g[h][:].bitcast(FP8X4), rhs_scale=c_plane[:, cols], start=False, stop=True)
-                part = sb.tile([P, HALF], F32, name=f"part{h}{j}")
-                nc.vector.scalar_tensor_tensor(part[:], acc[:], -2.0, kn_g[:, cols], ALU.mult, ALU.add)
                 res = sb.tile([P, HALF], F32, name=f"res{h}{j}")
-                nc.scalar.activation(res[:], part[:], ACT.Relu, bias=qn_cols[:, j : j + 1])
-                (nc.scalar if h + j == 2 else nc.sync).dma_start(out_v[:, j, cols], res[:])
+                for e in range(2):
+                    cols = slice((2 * h + e) * QUARTER, (2 * h + e + 1) * QUARTER)
+                    half_cols = slice(e * QUARTER, (e + 1) * QUARTER)
+                    acc = accs[h, j, e]
+                    nc.tensor.matmul_mx(out=acc[:], lhsT=q_codes[:, rows].bitcast(FP8X4), lhsT_scale=q_scales[:, rows],
+                                        rhs=cw_g[h][:, half_cols].bitcast(FP8X4), rhs_scale=c_plane[:, cols], start=False, stop=True)
+                    part = sb.tile([P, QUARTER], F32, name=f"part{h}{j}{e}")
+                    nc.vector.scalar_tensor_tensor(part[:], acc[:], -2.0, kn_g[:, cols], ALU.mult, ALU.add)
+                    nc.scalar.activation(res[:, half_cols], part[:], ACT.Relu, bias=qn_cols[:, j : j + 1])
+                (nc.scalar if h + j == 2 else nc.sync).dma_start(out_v[:, j, h * HALF : (h + 1) * HALF], res[:])

@@ -53,7 +53,7 @@ def tile_attend_residdist_topk_kernel(tc, qT, k_words, k_scales, c_words, c_scal
         nc.sync.dma_start(q_raw0[:], q_rows[:, 0:2, :])
         nc.scalar.dma_start(kn_cols[:], kn[0].rearrange("(p c) -> p c", c=KN_COLS))
         nc.sync.dma_start(offsets[:], offs)
-        nc.sync.dma_start(ks_win[0:P:8, :].bitcast(I32), k_scales[0].bitcast(I32))
+        nc.sync.dma_start(ks_win[32:96:4, :].bitcast(I32), k_scales[0].bitcast(I32))
         nc.sync.dma_start(q_raw1[:], q_rows[:, 2:4, :])
         nc.sync.dma_start(cs_win[4:P:8, :].bitcast(I32), c_scales[0].bitcast(I32))
         nc.sync.dma_start(kw_win[:], k_words[0].rearrange("p n t -> p (n t)").bitcast(I32))
@@ -63,7 +63,7 @@ def tile_attend_residdist_topk_kernel(tc, qT, k_words, k_scales, c_words, c_scal
         cs_g = sb.tile([P, N], U8, name="cs_g", align_bytes=64)
         nc.vector.tensor_copy(ks_g[:], ks_win[:].indirect(offsets[:]))
         for r in range(4):
-            nc.sync.dma_start(k_plane[r:P:32, :].bitcast(I32), ks_g[8 * r : P : 32, :].bitcast(I32))
+            nc.sync.dma_start(k_plane[r:P:32, :].bitcast(I32), ks_g[32 + 4 * r : 96 : 16, :].bitcast(I32))
         nc.sync.dma_start(cw_win[:, CW_FIRST:], cw_rows[:, CW_FIRST:])
         nc.vector.tensor_copy(cs_g[:], cs_win[:].indirect(offsets[:]))
         for r in range(4):
@@ -97,6 +97,10 @@ def tile_attend_residdist_topk_kernel(tc, qT, k_words, k_scales, c_words, c_scal
             g = sb.tile([P, HALF], U32, name=f"cw_g{h}", align_bytes=64)
             nc.vector.tensor_copy(g[:], cw_win[:].bitcast(U32).indirect(offsets[:, h * 16 : (h + 1) * 16]))
             cw_g.append(g)
+        for n in range(2):
+            warm = ps.tile([P, NQ], F32, name=f"warm{n}", tag=f"bank{n}")
+            nc.tensor.matmul_mx(out=warm[:], lhsT=q_codes[:, :P].bitcast(FP8X4), lhsT_scale=q_scales[:, :P],
+                                rhs=q_codes[:].bitcast(FP8X4), rhs_scale=q_scales[:], start=True, stop=True)
         QUARTER = N // 4
         pieces = [(h, j, e) for h in range(2) for j in range(2) for e in range(2)]
         accs = {}
@@ -120,4 +124,7 @@ def tile_attend_residdist_topk_kernel(tc, qT, k_words, k_scales, c_words, c_scal
                     part = sb.tile([P, QUARTER], F32, name=f"part{h}{j}{e}")
                     nc.vector.scalar_tensor_tensor(part[:], acc[:], -2.0, kn_g[:, cols], ALU.mult, ALU.add)
                     nc.scalar.activation(res[:, half_cols], part[:], ACT.Relu, bias=qn_cols[:, j : j + 1])
-                (nc.scalar if h + j == 2 else nc.sync).dma_start(out_v[:, j, h * HALF : (h + 1) * HALF], res[:])
+                    if h + j == 0:
+                        nc.sync.dma_start(out_v[:, j, cols], res[:, half_cols])
+                if h + j > 0:
+                    nc.sync.dma_start(out_v[:, j, h * HALF : (h + 1) * HALF], res[:])

@@ -97,10 +97,6 @@ def tile_attend_residdist_topk_kernel(tc, qT, k_words, k_scales, c_words, c_scal
             g = sb.tile([P, HALF], U32, name=f"cw_g{h}", align_bytes=64)
             nc.vector.tensor_copy(g[:], cw_win[:].bitcast(U32).indirect(offsets[:, h * 16 : (h + 1) * 16]))
             cw_g.append(g)
-        for n in range(2):
-            warm = ps.tile([P, NQ], F32, name=f"warm{n}", tag=f"bank{n}")
-            nc.tensor.matmul_mx(out=warm[:], lhsT=q_codes[:, :P].bitcast(FP8X4), lhsT_scale=q_scales[:, :P],
-                                rhs=q_codes[:].bitcast(FP8X4), rhs_scale=q_scales[:], start=True, stop=True)
         QUARTER = N // 4
         pieces = [(h, j, e) for h in range(2) for j in range(2) for e in range(2)]
         accs = {}

@@ -42,8 +42,8 @@ def tile_attend_residdist_topk_kernel(tc, qT, k_words, k_scales, c_words, c_scal
         c_plane = sb.tile([P, N], U8, name="c_plane", align_bytes=64)
         ident = sb.tile([P, P], F32, name="ident")
         nc.vector.memset(ks_win[:].bitcast(I32), 0)
-        nc.vector.memset(cs_win[:].bitcast(I32), 0)
         nc.vector.memset(ident[:], 0.0)
+        nc.vector.memset(cs_win[:].bitcast(I32), 0)
         nc.vector.memset(k_plane[:].bitcast(I32), 0)
         nc.vector.memset(c_plane[:].bitcast(I32), 0)
         nc.gpsimd.affine_select(out=ident[:], in_=ident[:], compare_op=ALU.not_equal, fill=1.0, base=0,

@@ -20,7 +20,6 @@ D = 512
 HALF = N // 2
 FLOPS = 2 * 2 * NQ * N * D
 CW_FIRST = 896
-KN_COLS = T // P
 
 
 def tile_attend_residdist_topk_kernel(tc, qT, k_words, k_scales, c_words, c_scales, kn, qn, offs, out):
@@ -34,24 +33,23 @@ def tile_attend_residdist_topk_kernel(tc, qT, k_words, k_scales, c_words, c_scal
         cs_win = sb.tile([P, T], U8, name="cs_win", align_bytes=64)
         kw_win = sb.tile([P, T], I32, name="kw_win", align_bytes=64)
         cw_win = sb.tile([P, T], I32, name="cw_win", align_bytes=64)
-        q_raw0 = sb.tile([P, 2, NQ], F32, name="q_raw0", tag="q_raw_then_kn_win", align_bytes=64)
+        q_raw0 = sb.tile([P, 2, NQ], F32, name="q_raw0", align_bytes=64)
         q_raw1 = sb.tile([P, 2, NQ], F32, name="q_raw1", align_bytes=64)
         qn_cols = sb.tile([P, 2], F32, name="qn_cols")
-        kn_cols = sb.tile([P, KN_COLS], F32, name="kn_cols")
+        kn_win = sb.tile([P, T], F32, name="kn_win", align_bytes=64)
         k_plane = sb.tile([P, N], U8, name="k_plane", align_bytes=64)
         c_plane = sb.tile([P, N], U8, name="c_plane", align_bytes=64)
         ident = sb.tile([P, P], F32, name="ident")
         nc.vector.memset(ks_win[:].bitcast(I32), 0)
-        nc.vector.memset(ident[:], 0.0)
         nc.vector.memset(cs_win[:].bitcast(I32), 0)
-        nc.vector.memset(k_plane[:].bitcast(I32), 0)
-        nc.vector.memset(c_plane[:].bitcast(I32), 0)
+        nc.vector.memset(kn_win[: P - 1, :].bitcast(I32), 0)
+        nc.vector.memset(ident[:], 0.0)
         nc.gpsimd.affine_select(out=ident[:], in_=ident[:], compare_op=ALU.not_equal, fill=1.0, base=0,
                                 pattern=[[-1, P]], channel_multiplier=1)
         q_rows = qT[0].rearrange("(p t) w -> p t w", t=4)
         cw_rows = c_words[0].rearrange("p n t -> p (n t)").bitcast(I32)
         nc.sync.dma_start(q_raw0[:], q_rows[:, 0:2, :])
-        nc.scalar.dma_start(kn_cols[:], kn[0].rearrange("(p c) -> p c", c=KN_COLS))
+        nc.scalar.dma_start(kn_win[P - 1 : P, :], kn[0:1, :])
         nc.sync.dma_start(offsets[:], offs)
         nc.sync.dma_start(ks_win[32:96:4, :].bitcast(I32), k_scales[0].bitcast(I32))
         nc.sync.dma_start(q_raw1[:], q_rows[:, 2:4, :])
@@ -61,10 +59,15 @@ def tile_attend_residdist_topk_kernel(tc, qT, k_words, k_scales, c_words, c_scal
 
         ks_g = sb.tile([P, N], U8, name="ks_g", align_bytes=64)
         cs_g = sb.tile([P, N], U8, name="cs_g", align_bytes=64)
+        kn_g = [sb.tile([P, HALF], F32, name=f"kn_g{h}", align_bytes=64) for h in range(2)]
+        nc.vector.memset(k_plane[:].bitcast(I32), 0)
         nc.vector.tensor_copy(ks_g[:], ks_win[:].indirect(offsets[:]))
         for r in range(4):
             nc.sync.dma_start(k_plane[r:P:32, :].bitcast(I32), ks_g[32 + 4 * r : 96 : 16, :].bitcast(I32))
         nc.sync.dma_start(cw_win[:, CW_FIRST:], cw_rows[:, CW_FIRST:])
+        nc.vector.tensor_copy(kn_g[0][:], kn_win[:].indirect(offsets[:, 0:16]))
+        nc.vector.tensor_copy(kn_g[1][:], kn_win[:].indirect(offsets[:, 16:32]))
+        nc.vector.memset(c_plane[:].bitcast(I32), 0)
         nc.vector.tensor_copy(cs_g[:], cs_win[:].indirect(offsets[:]))
         for r in range(4):
             nc.sync.dma_start(c_plane[r:P:32, :].bitcast(I32), cs_g[8 * r + 4 : P : 32, :].bitcast(I32))
@@ -77,19 +80,25 @@ def tile_attend_residdist_topk_kernel(tc, qT, k_words, k_scales, c_words, c_scal
         q_scales = sb.tile([P, NQ], U8, name="q_scales", align_bytes=64)
         nc.vector.quantize_mx(out=q_codes[:].bitcast(FP8X4), scales=q_scales[:], in_=q_bf[:].rearrange("p j m t -> p (j m t)"))
 
-        kn_win = sb.tile([P, T], F32, name="kn_win", tag="q_raw_then_kn_win", align_bytes=64)
-        kn_by_col = kn_win[:].rearrange("m (p c) -> m p c", c=KN_COLS)
-        for b in range(4):
-            bank = ps.tile([P, 4, P], F32, name=f"kn_bank{b}", tag=f"bank{b}")
-            for e in range(4):
-                c = 4 * b + e
-                nc.tensor.transpose(bank[:, e, :], kn_cols[:, c : c + 1].to_broadcast([P, P]), ident[:])
-            nc.scalar.copy(kn_by_col[:, :, 4 * b : 4 * b + 4], bank[:].rearrange("m e p -> m p e"))
+        kn_rows = []
+        for h in range(2):
+            turned = ps.tile([P, 2, P], F32, name=f"kn_turned{h}", tag=f"bank{2 * h}")
+            for e in range(2):
+                nc.tensor.transpose(turned[:, e, :], kn_g[h][:, e * P : (e + 1) * P], ident[:])
+            kn_col = sb.tile([P, 2], F32, name=f"kn_col{h}")
+            nc.scalar.copy(kn_col[:], turned[:, :, P - 1])
+            spread = ps.tile([P, 2, P], F32, name=f"kn_spread{h}", tag=f"bank{2 * h + 1}")
+            for e in range(2):
+                nc.tensor.transpose(spread[:, e, :], kn_col[:, e : e + 1].to_broadcast([P, P]), ident[:])
+            kn_row = sb.tile([P, HALF], F32, name=f"kn_row{h}")
+            nc.scalar.copy(kn_row[:], spread[:].rearrange("m e p -> m (e p)"))
+            kn_rows.append(kn_row)
 
-        kw_g = sb.tile([P, N], U32, name="kw_g", align_bytes=64)
-        nc.vector.tensor_copy(kw_g[:], kw_win[:].bitcast(U32).indirect(offsets[:]))
-        kn_g = sb.tile([P, N], F32, name="kn_g", align_bytes=64)
-        nc.vector.tensor_copy(kn_g[:], kn_win[:].indirect(offsets[:]))
+        kw_g = []
+        for h in range(2):
+            g = sb.tile([P, HALF], U32, name=f"kw_g{h}", align_bytes=64)
+            nc.vector.tensor_copy(g[:], kw_win[:].bitcast(U32).indirect(offsets[:, h * 16 : (h + 1) * 16]))
+            kw_g.append(g)
 
         out_v = out[0].rearrange("(m j) i -> m j i", j=2)
         cw_g = []
@@ -106,7 +115,7 @@ def tile_attend_residdist_topk_kernel(tc, qT, k_words, k_scales, c_words, c_scal
             acc = ps.tile([P, QUARTER], F32, name=f"acc{n}", tag=f"bank{(n + 4) % 8}")
             accs[h, j, e] = acc
             nc.tensor.matmul_mx(out=acc[:], lhsT=q_codes[:, rows].bitcast(FP8X4), lhsT_scale=q_scales[:, rows],
-                                rhs=kw_g[:, cols].bitcast(FP8X4), rhs_scale=k_plane[:, cols], start=True, stop=False)
+                                rhs=kw_g[h][:, e * QUARTER : (e + 1) * QUARTER].bitcast(FP8X4), rhs_scale=k_plane[:, cols], start=True, stop=False)
         for h in range(2):
             for j in range(2):
                 rows = slice(j * P, (j + 1) * P)
@@ -118,7 +127,7 @@ def tile_attend_residdist_topk_kernel(tc, qT, k_words, k_scales, c_words, c_scal
                     nc.tensor.matmul_mx(out=acc[:], lhsT=q_codes[:, rows].bitcast(FP8X4), lhsT_scale=q_scales[:, rows],
                                         rhs=cw_g[h][:, half_cols].bitcast(FP8X4), rhs_scale=c_plane[:, cols], start=False, stop=True)
                     part = sb.tile([P, QUARTER], F32, name=f"part{h}{j}{e}")
-                    nc.vector.scalar_tensor_tensor(part[:], acc[:], -2.0, kn_g[:, cols], ALU.mult, ALU.add)
+                    nc.vector.scalar_tensor_tensor(part[:], acc[:], -2.0, kn_rows[h][:, half_cols], ALU.mult, ALU.add)
                     nc.scalar.activation(res[:, half_cols], part[:], ACT.Relu, bias=qn_cols[:, j : j + 1])
                     if h + j == 0:
                         nc.sync.dma_start(out_v[:, j, cols], res[:, half_cols])

@@ -59,14 +59,11 @@ def tile_attend_residdist_topk_kernel(tc, qT, k_words, k_scales, c_words, c_scal
 
         ks_g = sb.tile([P, N], U8, name="ks_g", align_bytes=64)
         cs_g = sb.tile([P, N], U8, name="cs_g", align_bytes=64)
-        kn_g = [sb.tile([P, HALF], F32, name=f"kn_g{h}", align_bytes=64) for h in range(2)]
         nc.vector.memset(k_plane[:].bitcast(I32), 0)
         nc.vector.tensor_copy(ks_g[:], ks_win[:].indirect(offsets[:]))
         for r in range(4):
             nc.sync.dma_start(k_plane[r:P:32, :].bitcast(I32), ks_g[32 + 4 * r : 96 : 16, :].bitcast(I32))
         nc.sync.dma_start(cw_win[:, CW_FIRST:], cw_rows[:, CW_FIRST:])
-        nc.vector.tensor_copy(kn_g[0][:], kn_win[:].indirect(offsets[:, 0:16]))
-        nc.vector.tensor_copy(kn_g[1][:], kn_win[:].indirect(offsets[:, 16:32]))
         nc.vector.memset(c_plane[:].bitcast(I32), 0)
         nc.vector.tensor_copy(cs_g[:], cs_win[:].indirect(offsets[:]))
         for r in range(4):
@@ -80,19 +77,18 @@ def tile_attend_residdist_topk_kernel(tc, qT, k_words, k_scales, c_words, c_scal
         q_scales = sb.tile([P, NQ], U8, name="q_scales", align_bytes=64)
         nc.vector.quantize_mx(out=q_codes[:].bitcast(FP8X4), scales=q_scales[:], in_=q_bf[:].rearrange("p j m t -> p (j m t)"))
 
-        kn_rows = []
-        for h in range(2):
-            turned = ps.tile([P, 2, P], F32, name=f"kn_turned{h}", tag=f"bank{2 * h}")
-            for e in range(2):
-                nc.tensor.transpose(turned[:, e, :], kn_g[h][:, e * P : (e + 1) * P], ident[:])
-            kn_col = sb.tile([P, 2], F32, name=f"kn_col{h}")
-            nc.scalar.copy(kn_col[:], turned[:, :, P - 1])
-            spread = ps.tile([P, 2, P], F32, name=f"kn_spread{h}", tag=f"bank{2 * h + 1}")
-            for e in range(2):
-                nc.tensor.transpose(spread[:, e, :], kn_col[:, e : e + 1].to_broadcast([P, P]), ident[:])
-            kn_row = sb.tile([P, HALF], F32, name=f"kn_row{h}")
-            nc.scalar.copy(kn_row[:], spread[:].rearrange("m e p -> m (e p)"))
-            kn_rows.append(kn_row)
+        kn_g = sb.tile([P, N], F32, name="kn_g", align_bytes=64)
+        nc.scalar.activation(kn_g[:], kn_win[:].indirect(offsets[:]), ACT.Copy)
+        turned = ps.tile([P, 4, P], F32, name="kn_turned", tag="bank0")
+        for e in range(4):
+            nc.tensor.transpose(turned[:, e, :], kn_g[:, e * P : (e + 1) * P], ident[:])
+        kn_col = sb.tile([P, 4], F32, name="kn_col")
+        nc.scalar.copy(kn_col[:], turned[:, :, P - 1])
+        spread = ps.tile([P, 4, P], F32, name="kn_spread", tag="bank1")
+        for e in range(4):
+            nc.tensor.transpose(spread[:, e, :], kn_col[:, e : e + 1].to_broadcast([P, P]), ident[:])
+        kn_row = sb.tile([P, N], F32, name="kn_row")
+        nc.scalar.copy(kn_row[:], spread[:].rearrange("m e p -> m (e p)"))
 
         kw_g = []
         for h in range(2):
@@ -112,7 +108,7 @@ def tile_attend_residdist_topk_kernel(tc, qT, k_words, k_scales, c_words, c_scal
         for n, (h, j, e) in enumerate(pieces):
             cols = slice((2 * h + e) * QUARTER, (2 * h + e + 1) * QUARTER)
             rows = slice(j * P, (j + 1) * P)
-            acc = ps.tile([P, QUARTER], F32, name=f"acc{n}", tag=f"bank{(n + 4) % 8}")
+            acc = ps.tile([P, QUARTER], F32, name=f"acc{n}", tag=f"bank{(n + 2) % 8}")
             accs[h, j, e] = acc
             nc.tensor.matmul_mx(out=acc[:], lhsT=q_codes[:, rows].bitcast(FP8X4), lhsT_scale=q_scales[:, rows],
                                 rhs=kw_g[h][:, e * QUARTER : (e + 1) * QUARTER].bitcast(FP8X4), rhs_scale=k_plane[:, cols], start=True, stop=False)
@@ -127,7 +123,7 @@ def tile_attend_residdist_topk_kernel(tc, qT, k_words, k_scales, c_words, c_scal
                     nc.tensor.matmul_mx(out=acc[:], lhsT=q_codes[:, rows].bitcast(FP8X4), lhsT_scale=q_scales[:, rows],
                                         rhs=cw_g[h][:, half_cols].bitcast(FP8X4), rhs_scale=c_plane[:, cols], start=False, stop=True)
                     part = sb.tile([P, QUARTER], F32, name=f"part{h}{j}{e}")
-                    nc.vector.scalar_tensor_tensor(part[:], acc[:], -2.0, kn_rows[h][:, half_cols], ALU.mult, ALU.add)
+                    nc.vector.scalar_tensor_tensor(part[:], acc[:], -2.0, kn_row[:, cols], ALU.mult, ALU.add)
                     nc.scalar.activation(res[:, half_cols], part[:], ACT.Relu, bias=qn_cols[:, j : j + 1])
                     if h + j == 0:
                         nc.sync.dma_start(out_v[:, j, cols], res[:, half_cols])

@@ -19,7 +19,7 @@ NQ = 256
 D = 512
 HALF = N // 2
 FLOPS = 2 * 2 * NQ * N * D
-CW_FIRST = 896
+CW_FIRST = 1024
 
 
 def tile_attend_residdist_topk_kernel(tc, qT, k_words, k_scales, c_words, c_scales, kn, qn, offs, out):
@@ -33,8 +33,8 @@ def tile_attend_residdist_topk_kernel(tc, qT, k_words, k_scales, c_words, c_scal
         cs_win = sb.tile([P, T], U8, name="cs_win", align_bytes=64)
         kw_win = sb.tile([P, T], I32, name="kw_win", align_bytes=64)
         cw_win = sb.tile([P, T], I32, name="cw_win", align_bytes=64)
-        q_raw0 = sb.tile([P, 2, NQ], F32, name="q_raw0", align_bytes=64)
-        q_raw1 = sb.tile([P, 2, NQ], F32, name="q_raw1", align_bytes=64)
+        q_raw0 = sb.tile([P, 1, NQ], F32, name="q_raw0", align_bytes=64)
+        q_raw1 = sb.tile([P, 3, NQ], F32, name="q_raw1", align_bytes=64)
         qn_cols = sb.tile([P, 2], F32, name="qn_cols")
         kn_win = sb.tile([P, T], F32, name="kn_win", align_bytes=64)
         k_plane = sb.tile([P, N], U8, name="k_plane", align_bytes=64)
@@ -48,47 +48,51 @@ def tile_attend_residdist_topk_kernel(tc, qT, k_words, k_scales, c_words, c_scal
                                 pattern=[[-1, P]], channel_multiplier=1)
         q_rows = qT[0].rearrange("(p t) w -> p t w", t=4)
         cw_rows = c_words[0].rearrange("p n t -> p (n t)").bitcast(I32)
-        nc.sync.dma_start(q_raw0[:], q_rows[:, 0:2, :])
+        nc.sync.dma_start(q_raw0[:], q_rows[:, 0:1, :])
         nc.scalar.dma_start(kn_win[P - 1 : P, :], kn[0:1, :])
         nc.sync.dma_start(offsets[:], offs)
-        nc.sync.dma_start(ks_win[32:96:4, :].bitcast(I32), k_scales[0].bitcast(I32))
-        nc.sync.dma_start(q_raw1[:], q_rows[:, 2:4, :])
+        nc.sync.dma_start(ks_win[0:P:8, :].bitcast(I32), k_scales[0].bitcast(I32))
+        nc.sync.dma_start(q_raw1[:], q_rows[:, 1:4, :])
         nc.sync.dma_start(cs_win[4:P:8, :].bitcast(I32), c_scales[0].bitcast(I32))
         nc.sync.dma_start(kw_win[:], k_words[0].rearrange("p n t -> p (n t)").bitcast(I32))
         nc.sync.dma_start(cw_win[:, :CW_FIRST], cw_rows[:, :CW_FIRST])
 
         ks_g = sb.tile([P, N], U8, name="ks_g", align_bytes=64)
         cs_g = sb.tile([P, N], U8, name="cs_g", align_bytes=64)
-        nc.vector.memset(k_plane[:].bitcast(I32), 0)
         nc.vector.tensor_copy(ks_g[:], ks_win[:].indirect(offsets[:]))
-        for r in range(4):
-            nc.sync.dma_start(k_plane[r:P:32, :].bitcast(I32), ks_g[32 + 4 * r : 96 : 16, :].bitcast(I32))
+        nc.vector.tensor_copy(k_plane[:].bitcast(I32), ks_g[:].bitcast(I32))
+        for r in range(1, 4):
+            nc.sync.dma_start(k_plane[r:P:32, :].bitcast(I32), ks_g[8 * r : P : 32, :].bitcast(I32))
         nc.sync.dma_start(cw_win[:, CW_FIRST:], cw_rows[:, CW_FIRST:])
-        nc.vector.memset(c_plane[:].bitcast(I32), 0)
         nc.vector.tensor_copy(cs_g[:], cs_win[:].indirect(offsets[:]))
-        for r in range(4):
-            nc.sync.dma_start(c_plane[r:P:32, :].bitcast(I32), cs_g[8 * r + 4 : P : 32, :].bitcast(I32))
+        nc.vector.tensor_copy(c_plane[:].bitcast(I32), cs_g[:].bitcast(I32))
+        for r in range(1, 4):
+            nc.sync.dma_start(c_plane[4 + r : P : 32, :].bitcast(I32), cs_g[8 * r + 4 : P : 32, :].bitcast(I32))
         nc.sync.dma_start(qn_cols[:], qn[0].rearrange("(m j) o -> m (j o)", j=2))
 
         q_bf = sb.tile([P, 2, P, 4], BF16, name="q_bf", align_bytes=64)
-        for t0, q_raw in ((0, q_raw0), (2, q_raw1)):
-            nc.scalar.copy(q_bf[:, :, :, t0 : t0 + 2], q_raw[:].rearrange("p t (m j) -> p j m t", j=2))
+        for t0, t1, q_raw in ((0, 1, q_raw0), (1, 4, q_raw1)):
+            nc.scalar.copy(q_bf[:, :, :, t0:t1], q_raw[:].rearrange("p t (m j) -> p j m t", j=2))
         q_codes = sb.tile([P, NQ], U32, name="q_codes", align_bytes=64)
         q_scales = sb.tile([P, NQ], U8, name="q_scales", align_bytes=64)
         nc.vector.quantize_mx(out=q_codes[:].bitcast(FP8X4), scales=q_scales[:], in_=q_bf[:].rearrange("p j m t -> p (j m t)"))
 
-        kn_g = sb.tile([P, N], F32, name="kn_g", align_bytes=64)
-        nc.scalar.activation(kn_g[:], kn_win[:].indirect(offsets[:]), ACT.Copy)
-        turned = ps.tile([P, 4, P], F32, name="kn_turned", tag="bank0")
-        for e in range(4):
-            nc.tensor.transpose(turned[:, e, :], kn_g[:, e * P : (e + 1) * P], ident[:])
-        kn_col = sb.tile([P, 4], F32, name="kn_col")
-        nc.scalar.copy(kn_col[:], turned[:, :, P - 1])
-        spread = ps.tile([P, 4, P], F32, name="kn_spread", tag="bank1")
-        for e in range(4):
-            nc.tensor.transpose(spread[:, e, :], kn_col[:, e : e + 1].to_broadcast([P, P]), ident[:])
-        kn_row = sb.tile([P, N], F32, name="kn_row")
-        nc.scalar.copy(kn_row[:], spread[:].rearrange("m e p -> m (e p)"))
+        kn_g = [sb.tile([P, HALF], F32, name=f"kn_g{h}", align_bytes=64) for h in range(2)]
+        for h in range(2):
+            nc.scalar.activation(kn_g[h][:], kn_win[:].indirect(offsets[:, h * 16 : (h + 1) * 16]), ACT.Copy)
+        kn_rows = []
+        for h in range(2):
+            turned = ps.tile([P, 2, P], F32, name=f"kn_turned{h}", tag=f"bank{2 * h}")
+            for e in range(2):
+                nc.tensor.transpose(turned[:, e, :], kn_g[h][:, e * P : (e + 1) * P], ident[:])
+            kn_col = sb.tile([P, 2], F32, name=f"kn_col{h}")
+            nc.scalar.copy(kn_col[:], turned[:, :, P - 1])
+            spread = ps.tile([P, 2, P], F32, name=f"kn_spread{h}", tag=f"bank{2 * h + 1}")
+            for e in range(2):
+                nc.tensor.transpose(spread[:, e, :], kn_col[:, e : e + 1].to_broadcast([P, P]), ident[:])
+            kn_row = sb.tile([P, HALF], F32, name=f"kn_row{h}")
+            nc.scalar.copy(kn_row[:], spread[:].rearrange("m e p -> m (e p)"))
+            kn_rows.append(kn_row)
 
         kw_g = []
         for h in range(2):
@@ -108,7 +112,7 @@ def tile_attend_residdist_topk_kernel(tc, qT, k_words, k_scales, c_words, c_scal
         for n, (h, j, e) in enumerate(pieces):
             cols = slice((2 * h + e) * QUARTER, (2 * h + e + 1) * QUARTER)
             rows = slice(j * P, (j + 1) * P)
-            acc = ps.tile([P, QUARTER], F32, name=f"acc{n}", tag=f"bank{(n + 2) % 8}")
+            acc = ps.tile([P, QUARTER], F32, name=f"acc{n}", tag=f"bank{(n + 4) % 8}")
             accs[h, j, e] = acc
             nc.tensor.matmul_mx(out=acc[:], lhsT=q_codes[:, rows].bitcast(FP8X4), lhsT_scale=q_scales[:, rows],
                                 rhs=kw_g[h][:, e * QUARTER : (e + 1) * QUARTER].bitcast(FP8X4), rhs_scale=k_plane[:, cols], start=True, stop=False)
@@ -121,9 +125,9 @@ def tile_attend_residdist_topk_kernel(tc, qT, k_words, k_scales, c_words, c_scal
                     half_cols = slice(e * QUARTER, (e + 1) * QUARTER)
                     acc = accs[h, j, e]
                     nc.tensor.matmul_mx(out=acc[:], lhsT=q_codes[:, rows].bitcast(FP8X4), lhsT_scale=q_scales[:, rows],
-                                        rhs=cw_g[h][:, half_cols].bitcast(FP8X4), rhs_scale=c_plane[:, cols], start=False, stop=True)
+                                        rhs=cw_g[h][:, half_cols].bitcast(FP8X4), rhs_scale=c_plane[4:, cols], start=False, stop=True)
                     part = sb.tile([P, QUARTER], F32, name=f"part{h}{j}{e}")
-                    nc.vector.scalar_tensor_tensor(part[:], acc[:], -2.0, kn_row[:, cols], ALU.mult, ALU.add)
+                    nc.vector.scalar_tensor_tensor(part[:], acc[:], -2.0, kn_rows[h][:, half_cols], ALU.mult, ALU.add)
                     nc.scalar.activation(res[:, half_cols], part[:], ACT.Relu, bias=qn_cols[:, j : j + 1])
                     if h + j == 0:
                         nc.sync.dma_start(out_v[:, j, cols], res[:, half_cols])

from contextlib import ExitStack

import concourse.mybir as mybir

F32 = mybir.dt.float32
BF16 = mybir.dt.bfloat16
I32 = mybir.dt.int32
U32 = mybir.dt.uint32
U16 = mybir.dt.uint16
U8 = mybir.dt.uint8
FP8X4 = mybir.dt.float8_e4m3fn_x4
ALU = mybir.AluOpType
ACT = mybir.ActivationFunctionType

P = 128
T = 2048
N = 512
NQ = 256
D = 512
HALF = N // 2
FLOPS = 2 * 2 * NQ * N * D
CW_FIRST = 1024


def tile_attend_residdist_topk_kernel(tc, qT, k_words, k_scales, c_words, c_scales, kn, qn, offs, out):
    nc = tc.nc
    with ExitStack() as ctx:
        sb = ctx.enter_context(tc.tile_pool(name="sb", bufs=1))
        ps = ctx.enter_context(tc.psum_pool(name="ps", bufs=1))

        offsets = sb.tile([P, N // 16], U16, name="offsets")
        ks_win = sb.tile([P, T], U8, name="ks_win", align_bytes=64)
        cs_win = sb.tile([P, T], U8, name="cs_win", align_bytes=64)
        kw_win = sb.tile([P, T], I32, name="kw_win", align_bytes=64)
        cw_win = sb.tile([P, T], I32, name="cw_win", align_bytes=64)
        q_raw0 = sb.tile([P, 1, NQ], F32, name="q_raw0", align_bytes=64)
        q_raw1 = sb.tile([P, 3, NQ], F32, name="q_raw1", align_bytes=64)
        qn_cols = sb.tile([P, 2], F32, name="qn_cols")
        kn_win = sb.tile([P, T], F32, name="kn_win", align_bytes=64)
        k_plane = sb.tile([P, N], U8, name="k_plane", align_bytes=64)
        c_plane = sb.tile([P, N], U8, name="c_plane", align_bytes=64)
        ident = sb.tile([P, P], F32, name="ident")
        nc.vector.memset(ks_win[:].bitcast(I32), 0)
        nc.vector.memset(cs_win[:].bitcast(I32), 0)
        nc.vector.memset(kn_win[: P - 1, :].bitcast(I32), 0)
        nc.vector.memset(ident[:], 0.0)
        nc.gpsimd.affine_select(out=ident[:], in_=ident[:], compare_op=ALU.not_equal, fill=1.0, base=0,
                                pattern=[[-1, P]], channel_multiplier=1)
        q_rows = qT[0].rearrange("(p t) w -> p t w", t=4)
        cw_rows = c_words[0].rearrange("p n t -> p (n t)").bitcast(I32)
        nc.sync.dma_start(q_raw0[:], q_rows[:, 0:1, :])
        nc.scalar.dma_start(kn_win[P - 1 : P, :], kn[0:1, :])
        nc.sync.dma_start(offsets[:], offs)
        nc.sync.dma_start(ks_win[0:P:8, :].bitcast(I32), k_scales[0].bitcast(I32))
        nc.sync.dma_start(q_raw1[:], q_rows[:, 1:4, :])
        nc.sync.dma_start(cs_win[4:P:8, :].bitcast(I32), c_scales[0].bitcast(I32))
        nc.sync.dma_start(kw_win[:], k_words[0].rearrange("p n t -> p (n t)").bitcast(I32))
        nc.sync.dma_start(cw_win[:, :CW_FIRST], cw_rows[:, :CW_FIRST])

        ks_g = sb.tile([P, N], U8, name="ks_g", align_bytes=64)
        cs_g = sb.tile([P, N], U8, name="cs_g", align_bytes=64)
        nc.vector.tensor_copy(ks_g[:], ks_win[:].indirect(offsets[:]))
        nc.vector.tensor_copy(k_plane[:].bitcast(I32), ks_g[:].bitcast(I32))
        for r in range(1, 4):
            nc.sync.dma_start(k_plane[r:P:32, :].bitcast(I32), ks_g[8 * r : P : 32, :].bitcast(I32))
        nc.sync.dma_start(cw_win[:, CW_FIRST:], cw_rows[:, CW_FIRST:])
        nc.vector.tensor_copy(cs_g[:], cs_win[:].indirect(offsets[:]))
        nc.vector.tensor_copy(c_plane[:].bitcast(I32), cs_g[:].bitcast(I32))
        for r in range(1, 4):
            nc.sync.dma_start(c_plane[4 + r : P : 32, :].bitcast(I32), cs_g[8 * r + 4 : P : 32, :].bitcast(I32))
        nc.sync.dma_start(qn_cols[:], qn[0].rearrange("(m j) o -> m (j o)", j=2))

        q_bf = sb.tile([P, 2, P, 4], BF16, name="q_bf", align_bytes=64)
        for t0, t1, q_raw in ((0, 1, q_raw0), (1, 4, q_raw1)):
            nc.scalar.copy(q_bf[:, :, :, t0:t1], q_raw[:].rearrange("p t (m j) -> p j m t", j=2))
        q_codes = sb.tile([P, NQ], U32, name="q_codes", align_bytes=64)
        q_scales = sb.tile([P, NQ], U8, name="q_scales", align_bytes=64)
        nc.vector.quantize_mx(out=q_codes[:].bitcast(FP8X4), scales=q_scales[:], in_=q_bf[:].rearrange("p j m t -> p (j m t)"))

        kn_g = [sb.tile([P, HALF], F32, name=f"kn_g{h}", align_bytes=64) for h in range(2)]
        for h in range(2):
            nc.scalar.activation(kn_g[h][:], kn_win[:].indirect(offsets[:, h * 16 : (h + 1) * 16]), ACT.Copy)
        kn_rows = []
        for h in range(2):
            turned = ps.tile([P, 2, P], F32, name=f"kn_turned{h}", tag=f"bank{2 * h}")
            for e in range(2):
                nc.tensor.transpose(turned[:, e, :], kn_g[h][:, e * P : (e + 1) * P], ident[:])
            kn_col = sb.tile([P, 2], F32, name=f"kn_col{h}")
            nc.scalar.copy(kn_col[:], turned[:, :, P - 1])
            spread = ps.tile([P, 2, P], F32, name=f"kn_spread{h}", tag=f"bank{2 * h + 1}")
            for e in range(2):
                nc.tensor.transpose(spread[:, e, :], kn_col[:, e : e + 1].to_broadcast([P, P]), ident[:])
            kn_row = sb.tile([P, HALF], F32, name=f"kn_row{h}")
            nc.scalar.copy(kn_row[:], spread[:].rearrange("m e p -> m (e p)"))
            kn_rows.append(kn_row)

        kw_g = []
        for h in range(2):
            g = sb.tile([P, HALF], U32, name=f"kw_g{h}", align_bytes=64)
            nc.vector.tensor_copy(g[:], kw_win[:].bitcast(U32).indirect(offsets[:, h * 16 : (h + 1) * 16]))
            kw_g.append(g)

        out_v = out[0].rearrange("(m j) i -> m j i", j=2)
        cw_g = []
        for h in range(2):
            g = sb.tile([P, HALF], U32, name=f"cw_g{h}", align_bytes=64)
            nc.vector.tensor_copy(g[:], cw_win[:].bitcast(U32).indirect(offsets[:, h * 16 : (h + 1) * 16]))
            cw_g.append(g)
        QUARTER = N // 4
        pieces = [(h, j, e) for h in range(2) for j in range(2) for e in range(2)]
        accs = {}
        for n, (h, j, e) in enumerate(pieces):
            cols = slice((2 * h + e) * QUARTER, (2 * h + e + 1) * QUARTER)
            rows = slice(j * P, (j + 1) * P)
            acc = ps.tile([P, QUARTER], F32, name=f"acc{n}", tag=f"bank{(n + 4) % 8}")
            accs[h, j, e] = acc
            nc.tensor.matmul_mx(out=acc[:], lhsT=q_codes[:, rows].bitcast(FP8X4), lhsT_scale=q_scales[:, rows],
                                rhs=kw_g[h][:, e * QUARTER : (e + 1) * QUARTER].bitcast(FP8X4), rhs_scale=k_plane[:, cols], start=True, stop=False)
        for h in range(2):
            for j in range(2):
                rows = slice(j * P, (j + 1) * P)
                res = sb.tile([P, HALF], F32, name=f"res{h}{j}")
                for e in range(2):
                    cols = slice((2 * h + e) * QUARTER, (2 * h + e + 1) * QUARTER)
                    half_cols = slice(e * QUARTER, (e + 1) * QUARTER)
                    acc = accs[h, j, e]
                    nc.tensor.matmul_mx(out=acc[:], lhsT=q_codes[:, rows].bitcast(FP8X4), lhsT_scale=q_scales[:, rows],
                                        rhs=cw_g[h][:, half_cols].bitcast(FP8X4), rhs_scale=c_plane[4:, cols], start=False, stop=True)
                    part = sb.tile([P, QUARTER], F32, name=f"part{h}{j}{e}")
                    nc.vector.scalar_tensor_tensor(part[:], acc[:], -2.0, kn_rows[h][:, half_cols], ALU.mult, ALU.add)
                    nc.scalar.activation(res[:, half_cols], part[:], ACT.Relu, bias=qn_cols[:, j : j + 1])
                    if h + j == 0:
                        nc.sync.dma_start(out_v[:, j, cols], res[:, half_cols])
                if h + j > 0:
                    nc.sync.dma_start(out_v[:, j, h * HALF : (h + 1) * HALF], res[:])
